import numpy as np, ml_dtypes
CORES = [1,2,5,7,57,58,61,63,73,74,77,79]
N = 12
import mx_ref
NC, G = 256, 4
CNT = [[0,0,128,0,0,0,0,0,112,0,0,16],[0,16,0,128,0,0,0,0,0,0,0,112],[40,16,88,0,0,48,64,0,0,0,0,0],[40,0,0,8,112,0,80,0,0,16,0,0],[0,48,0,0,0,0,24,136,24,24,0,0],[0,64,0,0,0,0,72,0,0,0,120,0],[0,8,0,56,0,0,64,128,0,0,0,0],[0,0,0,48,16,0,0,104,0,8,0,80],[32,0,0,24,0,0,0,16,0,80,16,88],[120,104,0,16,0,0,0,0,0,0,16,0],[0,0,0,72,8,32,0,0,0,48,56,40],[40,0,0,0,32,56,0,0,0,72,56,0]]
OFF = [[sum(c[:e]) for e in range(N + 1)] for c in CNT]
TOT = [sum(c[e] for c in CNT) for e in range(N)]
C = np.float32(0.023)
BF = ml_dtypes.bfloat16
def cut(t, i, w=512):
    return t[:, w * i:w * i + w]
def tile(rs):
    return np.stack(rs, axis=2).reshape(128, -1).astype(BF)
def layer(w, X):
    out = []
    for i in range(G):
        for t in range(len(X)):
            p = mx_ref.matmul(mx_ref.quantize(cut(w, len(X) * i + t)), X[t])
            z = p if t == 0 else z + p
        out.append(z)
    return out
def act(Z):
    return [np.maximum(z, 0) * C for z in Z]
def setup_inputs(rng):
    def f(*shape):
        return mx_ref.flush((rng.standard_normal(shape, dtype=np.float32) * np.exp2(rng.integers(-2, 3, shape[:-1] + (1,)))).astype(BF))
    return {"x": f(N, 128, 4 * NC), "w1": f(N, 128, G * 512), "w2": f(N, 128, 512)}
def setup_inputs_blocks(rng):
    d = setup_inputs(rng)
    for k in ("x", "w1", "w2"): d[k] = mx_ref.spread(d[k], rng, 4)
    return d
def setup_inputs_wide(rng):
    d = setup_inputs(rng)
    for k in ("x", "w1", "w2"): d[k] = mx_ref.flush((d[k].astype(np.float32) * np.exp2(rng.integers(-8, 9, (N, 1, 1))).astype(np.float32)).astype(BF))
    return d
def setup_inputs_zeros(rng):
    d = setup_inputs(rng); v = d["x"].reshape(N, 128, -1, 4).copy()
    v[np.broadcast_to((rng.random((N, 1, v.shape[2], 1)) < 0.33), v.shape)] = 0
    d["x"] = v.reshape(d["x"].shape)
    return d
def reference(x, w1, w2):
    y = np.full((N, 128, max(TOT)), np.nan, np.float32)
    for e in range(N):
        t = np.concatenate([x[j][:, 4 * OFF[j][e]:4 * OFF[j][e + 1]] for j in range(N)], axis=1)
        y[e][:, :TOT[e]] = mx_ref.matmul(mx_ref.quantize(w2[e]), mx_ref.quantize(tile(act(layer(w1[e], [mx_ref.quantize(t)])))))
    return {"y": y}

from concourse.mybir import dt, AluOpType, ActivationFunctionType

NCOL = 256
HALF = 128
MINW = 128
NCH = 4
HW = 640
CSC = 0.023

RELAY_ON_RANK = True

SCRATCH = {
    "xt": ("sbuf", [128, 4 * NCOL], "bfloat16"),
    "w1t": ("sbuf", [128, 2048], "bfloat16"),
    "w2t": ("sbuf", [128, 512], "bfloat16"),
    "q": ("sbuf", [128, NCOL], "float8_e4m3fn_x4"),
    "qs": ("sbuf", [128, NCOL], "uint8"),
    "rl": ("sbuf", [128, NCOL], "float8_e4m3fn_x4"),
    "rls": ("sbuf", [128, NCOL], "uint8"),
    "bq": ("sbuf", [128, 384], "float8_e4m3fn_x4"),
    "bqs": ("sbuf", [128, 384], "uint8"),
    "w1q": ("sbuf", [128, 512], "float8_e4m3fn_x4"),
    "w1s": ("sbuf", [128, 512], "uint8"),
    "w2q": ("sbuf", [128, 128], "float8_e4m3fn_x4"),
    "w2s": ("sbuf", [128, 128], "uint8"),
    "h": ("sbuf", [128, 4 * HW], "bfloat16"),
    "hq": ("sbuf", [128, HW], "float8_e4m3fn_x4"),
    "hs": ("sbuf", [128, HW], "uint8"),
    "ysb": ("sbuf", [128, 384], "float32"),
    "ps": ("psum", [128, 4096], "float32"),
}
SEMAPHORES = (["xl0", "xl1", "wl0", "wl1", "wl2", "xq0", "xq1", "wq1", "wq2", "ys", "snt",
               "ar0", "ar1", "ar2", "rc0", "rc1", "rs0", "rs1"]
              + ["mm%d_%d" % (c, b) for c in range(NCH) for b in range(4)]
              + ["%s%d" % (s, c) for s in ("act", "hq", "m2_", "cp") for c in range(NCH)])


def _bits(mask):
    return [i for i in range(mask.bit_length()) if (mask >> i) & 1]


def _mk(bits):
    m = 0
    for b in bits:
        m |= 1 << b
    return m


def _halves(a, n):
    return sorted(set([a // HALF, (a + n - 1) // HALF]))


def _plan(T, topo):
    cores = list(T.cores)
    N = len(cores)
    CNT = T.tables["CNT"]
    OFF = [[sum(CNT[j][:e]) for e in range(N + 1)] for j in range(N)]
    TOT = [sum(CNT[j][e] for j in range(N)) for e in range(N)]
    YOFF = [[sum(CNT[i][e] for i in range(j)) for j in range(N)] for e in range(N)]
    pool = list(range(max(cores) + 1))

    def relay_for(s, d):
        cand = [c for c in pool if c != s and topo.chip(c) == topo.chip(s) and topo.may_write(c, d)]
        cand.sort(key=lambda c: ((c in cores) != RELAY_ON_RANK, topo.die(c) != topo.die(s), c))
        return cand[0]

    def masks(s, d, to_relay):
        allowed = _bits(topo.mask(s, d))
        if topo.chip(s) != topo.chip(d):
            return _mk(allowed), _mk(allowed), len(allowed), len(allowed)
        far = [f for f in pool if topo.chip(f) != topo.chip(s) and topo.may_write(s, f)][0]
        lo = [b for b in allowed if b in _bits(topo.mask(s, far))]
        hi = [b for b in allowed if b not in lo]
        sc = lo if to_relay else hi
        return _mk(hi), _mk(sc), len(hi), len(sc)

    pieces = [[] for _ in range(N)]
    blocks = []
    rlpos, rlnum = {}, {}
    for j in range(N):
        cur = None
        for e in range(N):
            n = CNT[j][e]
            if n == 0 or e == j:
                if e == j and n:
                    cur = None
                continue
            s, d = cores[j], cores[e]
            if topo.may_write(s, d):
                cls = 0 if topo.chip(s) == topo.chip(d) else 1
                pieces[e].append(dict(cls=cls, j=j, n=n, frm=s, src="q", a=OFF[j][e], blk=None))
                cur = None
                continue
            r = relay_for(s, d)
            if cur is None or cur["relay"] != r:
                cur = dict(j=j, relay=r, x0=OFF[j][e], n=0, pos=rlpos.get(r, 0), idx=rlnum.get(r, 0))
                rlnum[r] = cur["idx"] + 1
                blocks.append(cur)
            pieces[e].append(dict(cls=2, j=j, n=n, frm=r, src="rl", a=cur["pos"] + cur["n"], blk=cur))
            cur["n"] += n
            rlpos[r] = cur["pos"] + cur["n"]

    experts = []
    for e in range(N):
        ps = sorted(pieces[e], key=lambda p: (p["cls"], p["j"]))
        col = 0
        for p in ps:
            p["bcol"] = col
            col += p["n"]
        bch = []
        new0 = end = 0
        for cls in sorted(set(p["cls"] for p in ps)):
            end += sum(p["n"] for p in ps if p["cls"] == cls)
            if end >= MINW:
                st = min(new0, end - MINW)
                bch.append(dict(buf="bq", pbuf="bqs", start=st, n=end - st, new0=new0, end=end))
                new0 = end
        assert new0 == col
        for p in ps:
            p["k"] = [k for k, c in enumerate(bch) if c["new0"] <= p["bcol"] < c["end"]][0]
        chunks = []
        own = CNT[e][e]
        if own:
            wn = max(MINW, own)
            ws = min(OFF[e][e], NCOL - wn)
            chunks.append(dict(buf="q", pbuf="qs", start=ws, n=wn, waits=[("xq%d" % h, 1) for h in _halves(ws, wn)],
                               maps=[(OFF[e][e] - ws, YOFF[e][e], own)]))
        for k, c in enumerate(bch):
            c["maps"] = [(p["bcol"] - c["start"], YOFF[e][p["j"]], p["n"]) for p in ps if p["k"] == k]
            c["k"] = k
            chunks.append(c)
        comp = [-1] * TOT[e]
        for ci, c in enumerate(chunks):
            cp = []
            for (wo, yc, m) in sorted(c["maps"]):
                for t in range(yc, yc + m):
                    comp[t] = ci
                if cp and cp[-1][0] + cp[-1][2] == wo and cp[-1][1] + cp[-1][2] == yc:
                    cp[-1] = (cp[-1][0], cp[-1][1], cp[-1][2] + m)
                else:
                    cp.append((wo, yc, m))
            c["copies"] = cp
        assert min(comp) >= 0
        store = [-1] * TOT[e]
        for ci in range(len(chunks) - 1, -1, -1):
            mine = [t for t in range(TOT[e]) if comp[t] == ci and store[t] < 0]
            if mine:
                for t in range(min(mine), max(mine) + 1):
                    if store[t] < 0 and comp[t] <= ci:
                        store[t] = ci
        for ci, c in enumerate(chunks):
            iv = []
            for t in range(TOT[e]):
                if store[t] == ci:
                    if iv and iv[-1][1] == t:
                        iv[-1][1] = t + 1
                    else:
                        iv.append([t, t + 1])
            c["stores"] = iv
        experts.append(dict(chunks=chunks, nb=len(bch), last=bch[-1]["n"]))

    calls = {}
    arrive = [[0] * 3 for _ in range(N)]
    first_half = [0] * N
    for b in blocks:
        s = cores[b["j"]]
        mc, ms, kc, ks = masks(s, b["relay"], True)
        b["kc"], b["ks"] = kc, ks
        first_half[b["j"]] = b["x0"] // HALF
        calls.setdefault(s, []).append(dict(
            pr=(0, 0, -b["n"]), src="q", a=b["x0"], n=b["n"], dst=b["relay"], dbuf="rl", dcol=b["pos"],
            semc="rc%d" % b["idx"], sems="rs%d" % b["idx"], mc=mc, ms=ms, kc=kc, ks=ks,
            wc=[("xq%d" % h, 1) for h in _halves(b["x0"], b["n"])], ws=[]))
    for e in range(N):
        for p in pieces[e]:
            s, d = p["frm"], cores[e]
            mc, ms, kc, ks = masks(s, d, False)
            arrive[e][p["k"]] += kc + ks
            if p["blk"] is None:
                off = topo.chip(s) != topo.chip(d)
                pr = (1 if off else 2, 1 if off and topo.same_plane(topo.chip(s), topo.chip(d)) else 0, -p["n"])
                wc, ws = [("xq%d" % h, 1) for h in _halves(p["a"], p["n"])], []
            else:
                b = p["blk"]
                pr = (3, b["idx"], -experts[e]["last"], -p["n"])
                wc, ws = [("rc%d" % b["idx"], b["kc"])], [("rs%d" % b["idx"], b["ks"])]
            calls.setdefault(s, []).append(dict(
                pr=pr, src=p["src"], a=p["a"], n=p["n"], dst=d, dbuf="bq", dcol=p["bcol"],
                semc="ar%d" % p["k"], sems="ar%d" % p["k"], mc=mc, ms=ms, kc=kc, ks=ks, wc=wc, ws=ws))
    for c in calls:
        calls[c].sort(key=lambda x: x["pr"])
    for e in range(N):
        for c in experts[e]["chunks"]:
            if c["buf"] == "bq":
                c["waits"] = [("ar%d" % c["k"], arrive[e][c["k"]])]
    return dict(calls=calls, experts=experts, first_half=first_half)


def rank_program(g, core, T, topo):
    P = _plan(T, topo)
    S = T.sem
    rank = T.rank_of(core)
    u8 = dt.uint8

    if rank is not None:
        sy, sc, v, t = g.sync, g.scalar, g.vector, g.tensor
        hs = [P["first_half"][rank], 1 - P["first_half"][rank]]
        for i, (qu, h) in enumerate(zip((sy, sc), hs)):
            qu.dma_start(T.xt[:, 512 * h:512 * h + 512], T.x[:, 512 * h:512 * h + 512]).then_inc(S["xl%d" % i], 16)
        sy.dma_start(T.w1t[:, 0:1024], T.w1[:, 0:1024]).then_inc(S.wl0, 16)
        sc.dma_start(T.w1t[:, 1024:2048], T.w1[:, 1024:2048]).then_inc(S.wl1, 16)
        sy.dma_start(T.w2t[:], T.w2[:]).then_inc(S.wl2, 16)
        for i, h in enumerate(hs):
            v.wait_ge(S["xl%d" % i], 16)
            v.quantize_mx(T.q[:, HALF * h:HALF * h + HALF], T.qs[:, HALF * h:HALF * h + HALF],
                          T.xt[:, 512 * h:512 * h + 512]).then_inc(S["xq%d" % h], 1)
        for i in range(2):
            v.wait_ge(S["wl%d" % i], 16)
            v.quantize_mx(T.w1q[:, 256 * i:256 * i + 256], T.w1s[:, 256 * i:256 * i + 256],
                          T.w1t[:, 1024 * i:1024 * i + 1024]).then_inc(S.wq1, 1)
        v.wait_ge(S.wl2, 16)
        v.quantize_mx(T.w2q[:], T.w2s[:], T.w2t[:]).then_inc(S.wq2, 1)

        chunks = P["experts"][rank]["chunks"]
        ho = 0
        nst = 0
        for c, ch in enumerate(chunks):
            n, st, base = ch["n"], ch["start"], 4 * (c % 2)
            cod, pl = T[ch["buf"]], T[ch["pbuf"]]
            for nm, cnt in ch["waits"]:
                t.wait_ge(S[nm], cnt)
            if c == 0:
                t.wait_ge(S.wq1, 2)
            if c >= 2:
                t.wait_ge(S["act%d" % (c - 2)], 4)
                t.wait_ge(S["cp%d" % (c - 2)], len(chunks[c - 2]["copies"]))
            for b in range(4):
                z = T.ps[:, 512 * (base + b):512 * (base + b) + n]
                t.matmul_mx(z, T.w1q[:, 128 * b:128 * b + 128], T.w1s[:, 128 * b:128 * b + 128],
                            cod[:, st:st + n], pl[:, st:st + n], True, True).then_inc(S["mm%d_%d" % (c, b)], 1)
                hv = T.h[:, 4 * ho + b:4 * ho + 4 * n:4]
                if b % 2 == 0:
                    sc.wait_ge(S["mm%d_%d" % (c, b)], 1)
                    sc.activation(hv, z, ActivationFunctionType.Relu, scale=CSC).then_inc(S["act%d" % c], 1)
                else:
                    v.wait_ge(S["mm%d_%d" % (c, b)], 1)
                    v.tensor_scalar(hv, z, 0.0, CSC, AluOpType.max, AluOpType.mult).then_inc(S["act%d" % c], 1)
            v.wait_ge(S["act%d" % c], 4)
            v.quantize_mx(T.hq[:, ho:ho + n], T.hs[:, ho:ho + n], T.h[:, 4 * ho:4 * ho + 4 * n]).then_inc(S["hq%d" % c], 1)
            t.wait_ge(S["hq%d" % c], 1)
            if c == 0:
                t.wait_ge(S.wq2, 1)
            t.matmul_mx(T.ps[:, 512 * base:512 * base + n], T.w2q[:], T.w2s[:],
                        T.hq[:, ho:ho + n], T.hs[:, ho:ho + n], True, True).then_inc(S["m2_%d" % c], 1)
            sc.wait_ge(S["m2_%d" % c], 1)
            for wo, yc, m in ch["copies"]:
                sc.activation(T.ysb[:, yc:yc + m], T.ps[:, 512 * base + wo:512 * base + wo + m],
                              ActivationFunctionType.Copy).then_inc(S["cp%d" % c], 1)
            sy.wait_ge(S["cp%d" % c], len(ch["copies"]))
            for a, b in ch["stores"]:
                sy.dma_start(T.y[:, a:b], T.ysb[:, a:b]).then_inc(S.ys, 16)
                nst += 1
            ho += n
        sy.wait_ge(S.ys, 16 * nst)

    waited = set()
    sent = 0

    def need(lst):
        for nm, cnt in lst:
            if nm not in waited:
                g.wait_ge(S[nm], cnt)
                waited.add(nm)

    for c in P["calls"].get(core, []):
        rid, pid, _se = topo.addr(c["dst"])
        a, n, d = c["a"], c["n"], c["dcol"]
        need(c["wc"])
        g.remote_dma(T[c["dbuf"]][:, d:d + n].bitcast(u8), T[c["src"]][:, a:a + n].bitcast(u8),
                     S[c["semc"]], S.snt, pid, rid, c["mc"])
        need(c["ws"])
        g.remote_dma(T[c["dbuf"] + "s"][:, d:d + n], T[c["src"] + "s"][:, a:a + n],
                     S[c["sems"]], S.snt, pid, rid, c["ms"])
        sent += c["kc"] + c["ks"]
    if rank is not None:
        need([("xq0", 1), ("xq1", 1)])
    if sent:
        g.wait_ge(S.snt, sent)
